import numpy as np
import ml_dtypes

BF16 = ml_dtypes.bfloat16


def bf(x):
    return np.asarray(x, np.float32).astype(BF16)


def f32(x):
    return np.asarray(x, np.float32)


def f64(x):
    return np.asarray(x).astype(np.float64)


def striped(idx):
    return np.tile(idx.reshape(-1, 16).T, (8, 1))


def rows(idx, k):
    return np.tile(idx, (k, 1))


def look(tab, idx):
    return np.take_along_axis(f64(tab), rows(idx, len(tab)), axis=1)


K, S, V, N = 256, 4096, 2048, 2048


def setup_inputs():
    return {"tab": f32(np.random.standard_normal((K, S))), "y": f32(np.random.standard_normal((K, V))), "offs": striped(np.random.permutation(S)[:N])}


def reference(tab, y, offs):
    idx = offs[:16].T.reshape(-1)
    t = look(tab, idx)
    x = 1.0 / (1.0 + np.exp(-t)) * f64(y)
    return x

@@ -1,0 +1,34 @@
+import concourse.mybir as mybir
+
+F32 = mybir.dt.float32
+U16 = mybir.dt.uint16
+P = 128
+
+
+def tile_lookup_gate_sig_out_kernel(tc, tab, y, offs, out):
+    nc = tc.nc
+    rows, table_columns = tab.shape
+    list_length = y.shape[1]
+    blocks = rows // P
+
+    with (
+        tc.tile_pool(name="list", bufs=1) as list_pool,
+        tc.tile_pool(name="data", bufs=blocks) as data,
+    ):
+        offsets = list_pool.tile([P, list_length // 16], U16)
+        nc.sync.dma_start(offsets[:], offs)
+
+        for block in range(blocks):
+            block_rows = slice(block * P, (block + 1) * P)
+            table = data.tile([P, table_columns], F32)
+            stream = data.tile([P, list_length], F32)
+            gate = data.tile([P, list_length], F32)
+            product = data.tile([P, list_length], F32)
+
+            nc.sync.dma_start(table[:], tab[block_rows, :])
+            nc.sync.dma_start(stream[:], y[block_rows, :])
+            nc.scalar.activation(
+                gate[:], table[:].indirect(offsets[:]), mybir.ActivationFunctionType.Sigmoid
+            )
+            nc.vector.tensor_tensor(product[:], gate[:], stream[:], mybir.AluOpType.mult)
+            nc.sync.dma_start(out[block_rows, :], product[:])

@@ -3,32 +3,46 @@ import concourse.mybir as mybir
 F32 = mybir.dt.float32
 U16 = mybir.dt.uint16
 P = 128
+PIECE = 512
+AHEAD = 1024
 
 
 def tile_lookup_gate_sig_out_kernel(tc, tab, y, offs, out):
     nc = tc.nc
+    sigmoid = mybir.ActivationFunctionType.Sigmoid
+    mult = mybir.AluOpType.mult
     rows, table_columns = tab.shape
     list_length = y.shape[1]
     blocks = rows // P
 
     with (
         tc.tile_pool(name="list", bufs=1) as list_pool,
-        tc.tile_pool(name="data", bufs=blocks) as data,
+        tc.tile_pool(name="data", bufs=1) as data,
     ):
         offsets = list_pool.tile([P, list_length // 16], U16)
         nc.sync.dma_start(offsets[:], offs)
 
-        for block in range(blocks):
-            block_rows = slice(block * P, (block + 1) * P)
-            table = data.tile([P, table_columns], F32)
-            stream = data.tile([P, list_length], F32)
-            gate = data.tile([P, list_length], F32)
-            product = data.tile([P, list_length], F32)
+        tables = [data.tile([P, table_columns], F32, name=f"table{b}") for b in range(blocks)]
+        streams = [data.tile([P, list_length], F32, name=f"stream{b}") for b in range(blocks)]
+        gates = [data.tile([P, list_length], F32, name=f"gate{b}") for b in range(blocks)]
+        products = [data.tile([P, list_length], F32, name=f"product{b}") for b in range(blocks)]
 
-            nc.sync.dma_start(table[:], tab[block_rows, :])
-            nc.sync.dma_start(stream[:], y[block_rows, :])
-            nc.scalar.activation(
-                gate[:], table[:].indirect(offsets[:]), mybir.ActivationFunctionType.Sigmoid
-            )
-            nc.vector.tensor_tensor(product[:], gate[:], stream[:], mybir.AluOpType.mult)
-            nc.sync.dma_start(out[block_rows, :], product[:])
+        nc.sync.dma_start(tables[0][:], tab[0:P, :])
+        nc.sync.dma_start(streams[0][:, 0:AHEAD], y[0:P, 0:AHEAD])
+        nc.sync.dma_start(tables[1][:], tab[P : 2 * P, :])
+        nc.sync.dma_start(streams[0][:, AHEAD:], y[0:P, AHEAD:])
+        nc.sync.dma_start(streams[1][:], y[P : 2 * P, :])
+
+        for block in range(blocks):
+            for start in range(0, list_length, PIECE):
+                piece = slice(start, start + PIECE)
+                piece_offsets = offsets[:, start // 16 : (start + PIECE) // 16]
+                nc.scalar.activation(
+                    gates[block][:, piece], tables[block][:].indirect(piece_offsets), sigmoid
+                )
+                nc.vector.tensor_tensor(
+                    products[block][:, piece], gates[block][:, piece], streams[block][:, piece], mult
+                )
+                nc.sync.dma_start(
+                    out[block * P : (block + 1) * P, piece], products[block][:, piece]
+                )

@@ -22,6 +22,11 @@ def tile_lookup_gate_sig_out_kernel(tc, tab, y, offs, out):
         offsets = list_pool.tile([P, list_length // 16], U16)
         nc.sync.dma_start(offsets[:], offs)
 
+        warm_in = data.tile([P, 1], F32)
+        warm_out = data.tile([P, 1], F32)
+        nc.vector.memset(warm_in[:], 0.0)
+        nc.scalar.activation(warm_out[:], warm_in[:], sigmoid)
+
         tables = [data.tile([P, table_columns], F32, name=f"table{b}") for b in range(blocks)]
         streams = [data.tile([P, list_length], F32, name=f"stream{b}") for b in range(blocks)]
         gates = [data.tile([P, list_length], F32, name=f"gate{b}") for b in range(blocks)]

@@ -4,7 +4,6 @@ F32 = mybir.dt.float32
 U16 = mybir.dt.uint16
 P = 128
 PIECE = 512
-AHEAD = 1024
 
 
 def tile_lookup_gate_sig_out_kernel(tc, tab, y, offs, out):
@@ -33,9 +32,9 @@ def tile_lookup_gate_sig_out_kernel(tc, tab, y, offs, out):
         products = [data.tile([P, list_length], F32, name=f"product{b}") for b in range(blocks)]
 
         nc.sync.dma_start(tables[0][:], tab[0:P, :])
-        nc.sync.dma_start(streams[0][:, 0:AHEAD], y[0:P, 0:AHEAD])
+        nc.sync.dma_start(streams[0][:, 0:PIECE], y[0:P, 0:PIECE])
         nc.sync.dma_start(tables[1][:], tab[P : 2 * P, :])
-        nc.sync.dma_start(streams[0][:, AHEAD:], y[0:P, AHEAD:])
+        nc.sync.dma_start(streams[0][:, PIECE:], y[0:P, PIECE:])
         nc.sync.dma_start(streams[1][:], y[P : 2 * P, :])
 
         for block in range(blocks):

import concourse.mybir as mybir

F32 = mybir.dt.float32
U16 = mybir.dt.uint16
P = 128
PIECE = 512


def tile_lookup_gate_sig_out_kernel(tc, tab, y, offs, out):
    nc = tc.nc
    sigmoid = mybir.ActivationFunctionType.Sigmoid
    mult = mybir.AluOpType.mult
    rows, table_columns = tab.shape
    list_length = y.shape[1]
    blocks = rows // P

    with (
        tc.tile_pool(name="list", bufs=1) as list_pool,
        tc.tile_pool(name="data", bufs=1) as data,
    ):
        offsets = list_pool.tile([P, list_length // 16], U16)
        nc.sync.dma_start(offsets[:], offs)

        warm_in = data.tile([P, 1], F32)
        warm_out = data.tile([P, 1], F32)
        nc.vector.memset(warm_in[:], 0.0)
        nc.scalar.activation(warm_out[:], warm_in[:], sigmoid)

        tables = [data.tile([P, table_columns], F32, name=f"table{b}") for b in range(blocks)]
        streams = [data.tile([P, list_length], F32, name=f"stream{b}") for b in range(blocks)]
        gates = [data.tile([P, list_length], F32, name=f"gate{b}") for b in range(blocks)]
        products = [data.tile([P, list_length], F32, name=f"product{b}") for b in range(blocks)]

        nc.sync.dma_start(tables[0][:], tab[0:P, :])
        nc.sync.dma_start(streams[0][:, 0:PIECE], y[0:P, 0:PIECE])
        nc.sync.dma_start(tables[1][:], tab[P : 2 * P, :])
        nc.sync.dma_start(streams[0][:, PIECE:], y[0:P, PIECE:])
        nc.sync.dma_start(streams[1][:], y[P : 2 * P, :])

        for block in range(blocks):
            for start in range(0, list_length, PIECE):
                piece = slice(start, start + PIECE)
                piece_offsets = offsets[:, start // 16 : (start + PIECE) // 16]
                nc.scalar.activation(
                    gates[block][:, piece], tables[block][:].indirect(piece_offsets), sigmoid
                )
                nc.vector.tensor_tensor(
                    products[block][:, piece], gates[block][:, piece], streams[block][:, piece], mult
                )
                nc.sync.dma_start(
                    out[block * P : (block + 1) * P, piece], products[block][:, piece]
                )
